import numpy as np
import ml_dtypes


def mxq(x, axis, fmt="e4m3"):
    dtype, down = {"e4m3": (ml_dtypes.float8_e4m3fn, 7), "e5m2": (ml_dtypes.float8_e5m2, 14)}[fmt]
    v = np.moveaxis(np.asarray(x, np.float32).astype(ml_dtypes.bfloat16).astype(np.float64), axis, -1)
    blocks = v.reshape(v.shape[:-1] + (-1, 32))
    amax = np.abs(blocks).max(-1, keepdims=True)
    byte = np.maximum(np.where(amax > 0, np.frexp(amax)[1] - 1 + 127, 0) - down, 1)
    scale = np.exp2(byte - 127.0)
    codes = (blocks / scale).astype(np.float32).astype(dtype).astype(np.float64)
    return np.moveaxis((codes * scale).reshape(v.shape), -1, axis)


WIDE = False


def mx_kscale(k):
    if not WIDE:
        return np.ones(k)
    levels = np.array([10, -10, 5, -5, 0])
    if k % 512:
        return np.exp2(np.random.permutation(np.resize(levels, k // 32))).repeat(32)
    a = np.empty((k // 512, 16))
    for p in range(k // 512):
        a[p, :8] = np.random.permutation(np.resize(levels, 8))
        for g in range(8):
            far = levels[np.abs(levels - a[p, g]) >= 10]
            a[p, g + 8] = far[np.random.randint(len(far))]
    return np.exp2(a.ravel()).repeat(32)


def f64(x):
    return np.asarray(x).astype(np.float64)


def striped(idx):
    return np.tile(idx.reshape(-1, 16).T, (8, 1)).astype(np.uint16)


def unstriped(offs):
    return offs[:16].T.reshape(-1).astype(np.int64)


E2M1 = np.array([0.0, 0.5, 1.0, 1.5, 2.0, 3.0, 4.0, 6.0, -0.0, -0.5, -1.0, -1.5, -2.0, -3.0, -4.0, -6.0])


def pack_weight(w, fmt):
    k, n = w.shape
    w = f64(np.asarray(w, np.float32).astype(ml_dtypes.bfloat16)).reshape(k // 32, 32, n)
    amax = np.abs(w).max(1)
    if fmt == "e4m3":
        byte = np.frexp(amax)[1] - 1 + 127 - 7
    else:
        mant, ex = np.frexp(amax / 6.0)
        byte = np.where(mant > 0.5, ex, ex - 1) + 127
    byte = np.clip(np.where(amax > 0, byte, 1), 1, 254)
    scaled = (w * np.exp2(127.0 - byte)[:, None, :]).reshape(k, n).astype(np.float32)
    by_word = np.ascontiguousarray(scaled.reshape(k // 512, 128, 4, n).transpose(0, 1, 3, 2))
    if fmt == "e4m3":
        words = by_word.astype(ml_dtypes.float8_e4m3fn).view(np.uint8)
    else:
        c = by_word.astype(ml_dtypes.float4_e2m1fn).view(np.uint8) & 0xF
        words = (c[..., 0::2] | (c[..., 1::2] << 4)).reshape(k // 512, 128, 2 * n)
    return np.ascontiguousarray(words), np.ascontiguousarray(byte.astype(np.uint8).reshape(k // 512, 16, n))


def unpack_weight(words, scales, fmt):
    g, _, n = scales.shape
    words = np.ascontiguousarray(words).reshape(g, 128, n, -1)
    if fmt == "e4m3":
        vals = words.view(ml_dtypes.float8_e4m3fn).astype(np.float64)
    else:
        nib = np.empty((g, 128, n, 4), np.uint8)
        nib[..., 0::2] = words & 0xF
        nib[..., 1::2] = words >> 4
        vals = E2M1[nib]
    vals = vals * np.repeat(np.exp2(scales.astype(np.float64) - 127.0), 8, axis=1)[..., None]
    return vals.transpose(0, 1, 3, 2).reshape(g * 512, n)


def gelu(v):
    return 0.5 * v * (1.0 + np.tanh(np.sqrt(2.0 / np.pi) * (v + 0.044715 * v**3)))


def bf(x):
    return np.asarray(x, np.float32).astype(ml_dtypes.bfloat16)


def planes(Y):
    n, m = Y.shape
    b = f64(bf(Y)).reshape(n // 32, 32, m)
    amax = np.abs(b).max(1)
    byte = np.clip(np.where(amax > 0, np.frexp(amax)[1] - 1 + 127 - 7, 1), 1, 254)
    codes = (b * np.exp2(127.0 - byte)[:, None, :]).reshape(n, m).astype(np.float32).astype(ml_dtypes.float8_e4m3fn).view(np.uint8)
    words = codes.reshape(n // 512, 128, 4, m).transpose(0, 1, 3, 2)
    return np.ascontiguousarray(words), np.ascontiguousarray(byte.astype(np.uint8).reshape(n // 512, 16, m))


K, T, S, H, T2, P, N = 1024, 2048, 512, 1024, 1024, 512, 512

def setup_inputs():
    n = np.random.standard_normal
    s = mx_kscale(K)[:, None]
    u = mx_kscale(H)[:, None]
    size = np.exp(0.8 * n(N))
    tab_words, tab_scales = pack_weight(n((K, T)) * s, "e4m3")
    w3_words, w3_scales = pack_weight(0.7 * n((K, H)) / np.sqrt(K) / s, "e2m1")
    w4_words, w4_scales = pack_weight(n((H, N)) / np.sqrt(H) / u * size, "e4m3")
    return {
        "tab_words": tab_words, "tab_scales": tab_scales,
        "offs": striped(np.random.permutation(T)[:S]),
        "offs2": striped(np.random.permutation(T2)[:S]),
        "offs3": striped(np.random.permutation(T2)[:P]),
        "offs4": striped(np.random.permutation(T2)[:P]),
        "w1": (1.8 * n((K, H)) / np.sqrt(K) / s).astype(np.float32),
        "w2": (n((K, H)) / np.sqrt(K) / s).astype(np.float32),
        "w3_words": w3_words, "w3_scales": w3_scales,
        "gain": (1.4 * np.exp(0.3 * n(H)) * u[:, 0]).astype(np.float32),
        "wgs": np.exp(0.3 * n((128, S))).astype(np.float32),
        "page0": (0.7 * n((H, T2)) * u).astype(np.float32),
        "w4_words": w4_words, "w4_scales": w4_scales,
        "b4": (0.5 * n(N) * size).astype(np.float32),
    }

def reference(tab_words, tab_scales, offs, offs2, offs3, offs4, w1, w2, w3_words, w3_scales,
              gain, wgs, page0, w4_words, w4_scales, b4):
    v = unpack_weight(tab_words, tab_scales, "e4m3")[:, unstriped(offs)]
    h1 = mxq(f64(w1), 0, "e4m3").T @ v
    h2 = mxq(f64(w2), 0, "e4m3").T @ v
    h3 = unpack_weight(w3_words, w3_scales, "e2m1").T @ v
    h = f64(gain)[:, None] * (np.maximum(np.tanh(h1), h2) + h3)
    before = f64(page0)
    page = before.copy()
    page[:, unstriped(offs2)] = np.tile(f64(wgs), (H // 128, 1)) * h
    x = page[:, unstriped(offs3)] - before[:, unstriped(offs4)]
    xq = mxq(x, 0, "e4m3")
    y = (unpack_weight(w4_words, w4_scales, "e4m3").T @ xq) + f64(b4)[:, None]
    words, scales = planes(y)
    return y, words, scales

@@ -1,0 +1,406 @@
+from contextlib import ExitStack
+
+import concourse.mybir as mybir
+from concourse.masks import make_identity
+
+K, T, S, H, T2, M, N = 1024, 2048, 512, 1024, 1024, 512, 512
+FLOPS = 2 * (3 * K * H * S + H * N * M)
+
+F32 = mybir.dt.float32
+BF16 = mybir.dt.bfloat16
+I32 = mybir.dt.int32
+U32 = mybir.dt.uint32
+U16 = mybir.dt.uint16
+U8 = mybir.dt.uint8
+FP8X4 = mybir.dt.float8_e4m3fn_x4
+FP4X4 = mybir.dt.float4_e2m1fn_x4
+ALU = mybir.AluOpType
+ACT = mybir.ActivationFunctionType
+
+P = 128
+PACK = 4
+KP = P * PACK
+PASSES = K // KP
+QUAD = 32
+HALF_M = M // 2
+
+
+def tile_list_waterhole_redistribution_features_kernel(
+    tc, tab_words, tab_scales, offs, offs2, offs3, offs4, w1, w2, w3_words, w3_scales,
+    gain, wgs, page0, w4_words, w4_scales, b4, out_0, out_1, out_2,
+):
+    nc = tc.nc
+    with ExitStack() as ctx:
+        lists = ctx.enter_context(tc.tile_pool(name="lists", bufs=1))
+        pool = ctx.enter_context(tc.tile_pool(name="sbuf", bufs=1))
+        psum = ctx.enter_context(tc.psum_pool(name="psum", bufs=2))
+
+        def sb(name, shape, dtype, tag=None):
+            return pool.tile(shape, dtype, name=name, tag=tag or name, align_bytes=64)
+
+        def bank(name, tag, shape):
+            return psum.tile(shape, F32, name=name, tag=tag)
+
+        def load_list(name, src):
+            t = lists.tile([P, S // 16], U16, name=name)
+            nc.sync.dma_start(t[:], src)
+            return t
+
+        def load_weight_piece(name, w, a, col0, width):
+            raw = sb(name, [P, PACK, width], F32)
+            rows = w[a * KP : (a + 1) * KP, col0 : col0 + width]
+            nc.sync.dma_start(out=raw[:], in_=rows.rearrange("(p j) c -> p j c", j=PACK))
+            return raw
+
+        def load_page(name, rows):
+            t = sb(name, [P, T2], F32)
+            nc.sync.dma_start(out=t[:], in_=rows)
+            return t
+
+        def zero_plane(engine, name, width):
+            plane = sb(name, [P, PASSES, width], U8)
+            engine.memset(plane[:].bitcast(I32), 0)
+            return plane
+
+        def load_scales(queue, plane, src):
+            for q in range(P // QUAD):
+                queue.dma_start(
+                    out=plane[QUAD * q : QUAD * q + 4, :, :].bitcast(I32),
+                    in_=src[:, 4 * q : 4 * q + 4, :].rearrange("a r c -> r a c").bitcast(I32),
+                )
+
+        def interleave(engine_copy, dst, src):
+            engine_copy(
+                out=dst.rearrange("p (c i t) -> p c t i", i=4, t=PACK),
+                in_=src.rearrange("p t (c i) -> p c t i", i=4),
+            )
+
+        tab_plane = zero_plane(nc.gpsimd, "tab_plane", T)
+        w3_plane = zero_plane(nc.vector, "w3_plane", H)
+        w4_plane = zero_plane(nc.vector, "w4_plane", N)
+        load_scales(nc.scalar, tab_plane, tab_scales)
+        load_scales(nc.gpsimd, w3_plane, w3_scales)
+        gain_nat = sb("gain_nat", [P, PACK], F32)
+        with nc.allow_non_contiguous_dma(reason="one gain a partition"):
+            nc.gpsimd.dma_start(out=gain_nat[:], in_=gain[0:KP].rearrange("(b p) -> p b", p=P))
+
+        def load_table(a):
+            t = sb(f"tabw{a}", [P, T], I32)
+            nc.sync.dma_start(out=t[:], in_=tab_words[a].rearrange("p c i -> p (c i)").bitcast(I32))
+            return t
+
+        raw = {}
+
+        def load_chunk(c, which, col0, width):
+            for wi in which:
+                for a in range(PASSES):
+                    raw[c, wi, a] = load_weight_piece(f"raw{c}_{wi}{a}", (w1, w2)[wi], a, col0, width)
+
+        idx = load_list("idx", offs)
+        load_chunk(0, (0,), 0, P)
+        tabw = [load_table(0)]
+        load_chunk(0, (1,), 0, P)
+        tabw.append(load_table(1))
+        w3_codes = sb("w3_codes", [P, PASSES, 2 * H], U8)
+        nc.sync.dma_start(out=w3_codes[:].bitcast(I32), in_=w3_words.rearrange("a p c -> p a c").bitcast(I32))
+        page = [load_page("page0", page0[0:P, :])]
+        wgs_nat = sb("wgs_nat", [P, S], F32)
+        nc.sync.dma_start(out=wgs_nat[:], in_=wgs)
+        idx4 = load_list("idx4", offs4)
+        idx2 = load_list("idx2", offs2)
+        load_chunk(1, (0, 1), P, P)
+        idx3 = load_list("idx3", offs3)
+        page.append(load_page("page1", page0[P : 2 * P, :]))
+        load_chunk(2, (0, 1), 2 * P, 2 * P)
+        page.append(load_page("page2", page0[2 * P : 3 * P, :]))
+        load_chunk(3, (0,), KP, KP)
+        page.append(load_page("page3", page0[3 * P : 4 * P, :]))
+        load_chunk(3, (1,), KP, KP)
+        page_hi = page0[KP:H, :].rearrange("(p t) c -> p t c", t=PACK)
+        page.append(load_page("page4", page_hi[:, 0, :]))
+        wgs_dealt = sb("wgs_dealt", [P, PACK, S], F32)
+        for q in range(P // QUAD):
+            nc.sync.dma_start(
+                out=wgs_dealt[QUAD * q : QUAD * (q + 1), :, :],
+                in_=wgs.rearrange("(q t) j -> q t j", t=PACK),
+            )
+        for t in range(1, PACK):
+            page.append(load_page(f"page{4 + t}", page_hi[:, t, :]))
+        gain_dealt = sb("gain_dealt", [P, PACK], F32)
+        nc.sync.dma_start(out=gain_dealt[:], in_=gain[KP:H].rearrange("(p t) -> p t", t=PACK))
+        w4_raw = sb("w4_raw", [P, PASSES, N], I32)
+        nc.sync.dma_start(out=w4_raw[:], in_=w4_words.rearrange("a p c i -> p a (c i)").bitcast(I32))
+        load_scales(nc.sync, w4_plane, w4_scales)
+        b4_dealt = sb("b4_dealt", [P, PACK], F32)
+        nc.sync.dma_start(out=b4_dealt[:], in_=b4.rearrange("(p t) -> p t", t=PACK))
+
+        ident = sb("ident", [P, P], F32)
+        make_identity(nc, ident[:])
+
+        vw, vs = [], []
+        for a in range(PASSES):
+            s_t = sb(f"vs{a}", [P, S], U8)
+            nc.vector.tensor_copy(s_t[:], tab_plane[:, a, :].indirect(idx[:]))
+            w_t = sb(f"vw{a}", [P, S], U32)
+            nc.vector.tensor_copy(w_t[:], tabw[a][:].bitcast(U32).indirect(idx[:]))
+            vw.append(w_t)
+            vs.append(s_t)
+
+        codes, planes = {}, {}
+
+        def new_operands(c, which, width, tag):
+            words = sb(f"codes{c}_{which[0]}", [P, len(which), PASSES, width], U32, tag=tag)
+            plane = sb(f"planes{c}_{which[0]}", [P, len(which), PASSES, width], U8)
+            flat = "p w a c -> p (w a c)"
+            for n, wi in enumerate(which):
+                for a in range(PASSES):
+                    start = (PASSES * n + a) * width
+                    codes[c, wi, a] = (words[:].rearrange(flat), start)
+                    planes[c, wi, a] = (plane[:].rearrange(flat), start)
+
+        def quantise(c, width, pieces):
+            tag = f"stage{c}_{pieces[0][0]}{pieces[0][1]}"
+            stage = sb(tag, [P, len(pieces), PACK * width], BF16)
+            for n, (wi, a) in enumerate(pieces):
+                interleave(nc.scalar.copy, stage[:, n, :], raw[c, wi, a][:])
+            words, start = codes[(c,) + pieces[0]]
+            plane, start = planes[(c,) + pieces[0]]
+            span = slice(start, start + len(pieces) * width)
+            nc.vector.quantize_mx(
+                out=words[:, span].bitcast(FP8X4), scales=plane[:, span], in_=stage[:].rearrange("p n c -> p (n c)")
+            )
+            return tag
+
+        def product(out, stationary, moving):
+            for a in range(PASSES):
+                lw, ls = stationary(a)
+                rw, rs = moving(a)
+                nc.tensor.matmul_mx(
+                    out=out, lhsT=lw, lhsT_scale=ls, rhs=rw, rhs_scale=rs,
+                    start=(a == 0), stop=(a == PASSES - 1),
+                )
+
+        def table(cols):
+            return lambda a: (vw[a][:, cols].bitcast(FP8X4), vs[a][:, cols])
+
+        def weight(c, wi, cols):
+            def operand(a):
+                words, start = codes[c, wi, a]
+                plane, start = planes[c, wi, a]
+                span = slice(start + cols.start, start + cols.stop)
+                return words[:, span].bitcast(FP8X4), plane[:, span]
+
+            return operand
+
+        def weight3(col0, width):
+            return lambda a: (
+                w3_codes[:, a, 2 * col0 : 2 * (col0 + width)].bitcast(FP4X4),
+                w3_plane[:, a, col0 : col0 + width],
+            )
+
+        everything = slice(0, S)
+
+        h_lo = {}
+
+        def products_lo(b, c, col0):
+            cols = slice(col0, col0 + P)
+            h1 = bank(f"h1_{b}", "bank_a", [P, S])
+            product(h1[:], weight(c, 0, cols), table(everything))
+            h3 = bank(f"h3_{b}", "bank_c", [P, S])
+            product(h3[:], weight3(P * b, P), table(everything))
+            h2 = bank(f"h2_{b}", "bank_b", [P, S])
+            product(h2[:], weight(c, 1, cols), table(everything))
+            rec = sb(f"rec{b}", [P, S], F32)
+            nc.scalar.activation(rec[:], h1[:], ACT.Tanh)
+            wg = sb(f"wg{b}", [P, S], F32)
+            nc.scalar.activation(wg[:], wgs_nat[:], ACT.Copy, scale=gain_nat[:, b : b + 1])
+            h_lo[b] = (rec, h2, h3, wg)
+
+        def put_lo(b):
+            rec, h2, h3, wg = h_lo[b]
+            nc.vector.tensor_tensor(rec[:], rec[:], h2[:], ALU.max)
+            nc.vector.tensor_tensor(rec[:], rec[:], h3[:], ALU.add)
+            nc.vector.tensor_tensor(page[b][:].indirect(idx2[:]), rec[:], wg[:], ALU.mult)
+
+        def fetch_before(dst, b):
+            nc.vector.tensor_copy(dst, page[b][:].indirect(idx4[:]))
+
+        def fetch_difference(dst, b, before, lists_cols):
+            nc.vector.tensor_tensor(dst, page[b][:].indirect(idx3[:, lists_cols]), before, ALU.subtract)
+
+        all_cols = slice(0, M // 16)
+
+        new_operands(0, (0, 1), P, None)
+        for wi in range(2):
+            for a in range(PASSES):
+                quantise(0, P, [(wi, a)])
+        products_lo(0, 0, 0)
+        before0 = sb("before0", [P, M], F32)
+        fetch_before(before0[:], 0)
+        before = {0: before0[:]}
+        put_lo(0)
+
+        h3_hi = []
+        for jb in range(S // P):
+            acc = bank(f"h3t_{jb}", "bank_s", [P, KP])
+            product(acc[:], table(slice(P * jb, P * (jb + 1))), weight3(KP, KP))
+            c3 = sb(f"h3_hi{jb}", [P, PACK, P], F32, tag=f"raw0_{jb // 2}{jb % 2}")
+            nc.scalar.copy(out=c3[:], in_=acc[:].rearrange("p (q t) -> p t q", t=PACK))
+            h3_hi.append(c3)
+
+        x_lo = {}
+
+        def close_lo(b, tag):
+            pair = sb(f"pair{b}", [P, 2, M], F32, tag=tag)
+            fetch_difference(pair[:, 0, :], b, before[b], all_cols)
+            fetch_before(pair[:, 1, :], b + 1)
+            before[b + 1] = pair[:, 1, :]
+            x_lo[b] = pair
+
+        new_operands(1, (0, 1), P, "wg0")
+        tag = quantise(1, P, [(0, 0), (0, 1), (1, 0), (1, 1)])
+        products_lo(1, 1, 0)
+        close_lo(0, tag)
+        put_lo(1)
+
+        new_operands(2, (0, 1), 2 * P, "wg1")
+        quantise(2, 2 * P, [(0, 0), (0, 1)])
+        tag = quantise(2, 2 * P, [(1, 0), (1, 1)])
+        products_lo(2, 2, 0)
+        products_lo(3, 2, P)
+        close_lo(1, tag)
+        put_lo(2)
+
+        new_operands(3, (0,), KP, "wg2")
+        quantise(3, KP, [(0, 0)])
+        tag = quantise(3, KP, [(0, 1)])
+        tanh_tags = ["raw1_00", "raw1_01", "raw1_10", "raw2_00"]
+        tanh_hi = []
+        for jb in range(S // P):
+            acc = bank(f"h1t_{jb}", "bank_a", [P, KP])
+            product(acc[:], table(slice(P * jb, P * (jb + 1))), weight(3, 0, slice(0, KP)))
+            th = sb(f"tanh_hi{jb}", [P, PACK, P], F32, tag=tanh_tags[jb])
+            nc.scalar.activation(th[:], acc[:].rearrange("p (q t) -> p t q", t=PACK), ACT.Tanh)
+            tanh_hi.append(th)
+        close_lo(2, tag)
+        put_lo(3)
+
+        new_operands(3, (1,), KP, "wg3")
+        quantise(3, KP, [(1, 0)])
+        tag = quantise(3, KP, [(1, 1)])
+        close_lo(3, tag)
+        max_tags = ["raw1_11", "raw2_01", "raw2_10", "raw2_11"]
+        max_hi = []
+        for jb in range(S // P):
+            acc = bank(f"h2t_{jb}", ("bank_b", "bank_a")[jb % 2], [P, KP])
+            product(acc[:], table(slice(P * jb, P * (jb + 1))), weight(3, 1, slice(0, KP)))
+            mx = sb(f"max_hi{jb}", [P, PACK, P], F32, tag=max_tags[jb])
+            nc.vector.tensor_tensor(mx[:], tanh_hi[jb][:], acc[:].rearrange("p (q t) -> p t q", t=PACK), ALU.max)
+            max_hi.append(mx)
+
+        rec_hi = []
+        for t in range(PACK):
+            acc = bank(f"sum_{t}", "bank_s", [P, S])
+            terms = [(src, jb) for src in (h3_hi, max_hi) for jb in range(S // P)]
+            for n, (src, jb) in enumerate(terms):
+                nc.tensor.matmul(
+                    acc[:, P * jb : P * (jb + 1)], src[jb][:, t, :], ident[:],
+                    start=(n == 0), stop=(n == len(terms) - 1), is_transpose=True,
+                )
+            rec = sb(f"rec_hi{t}", [P, S], F32, tag=f"rec{t}")
+            nc.scalar.activation(rec[:], acc[:], ACT.Copy, scale=gain_dealt[:, t : t + 1])
+            rec_hi.append(rec)
+
+        pair56 = sb("pair56", [P, 2, M], F32, tag=tanh_tags[3])
+        for n in range(2):
+            fetch_before(pair56[:, n, :], 5 + n)
+            before[5 + n] = pair56[:, n, :]
+
+        w4_codes = sb("w4_codes", [P, PASSES, PACK, P], I32)
+        nc.vector.tensor_copy(
+            out=w4_codes[:].rearrange("p a t q -> p a q t"),
+            in_=w4_raw[:].rearrange("p a (q t) -> p a q t", t=PACK),
+        )
+        w4_dealt = sb("w4_dealt", [P, PASSES, PACK, P], U8)
+        nc.vector.tensor_copy(
+            out=w4_dealt[:].rearrange("p a t q -> p a q t"),
+            in_=w4_plane[:].rearrange("p a (q t) -> p a q t", t=PACK),
+        )
+
+        x_hi = sb("x_hi", [P, PACK, M], F32, tag="raw3_01")
+
+        def put_hi(t):
+            nc.vector.tensor_tensor(page[4 + t][:].indirect(idx2[:]), rec_hi[t][:], wgs_dealt[:, t, :], ALU.mult)
+
+        for t in range(PACK - 1):
+            put_hi(t)
+            fetch_difference(x_hi[:, t, :], 4 + t, before[4 + t], all_cols)
+
+        x_moved = sb("x_moved", [P, PACK, M], F32, tag="raw3_00")
+        for b in range(PACK):
+            for t in range(PACK):
+                nc.sync.dma_start(out=x_moved[QUAD * b : QUAD * (b + 1), t, :], in_=x_lo[b][t:P:PACK, 0, :])
+        x0_bf = sb("x0_bf", [P, PACK * M], BF16, tag=max_tags[3])
+        interleave(nc.scalar.copy, x0_bf[:], x_moved[:])
+        x0_codes = sb("x0_codes", [P, M], U32)
+        x0_plane = sb("x0_plane", [P, M], U8)
+        nc.vector.quantize_mx(out=x0_codes[:].bitcast(FP8X4), scales=x0_plane[:], in_=x0_bf[:])
+
+        before7 = sb("before7", [P, M], F32, tag=max_tags[3])
+        fetch_before(before7[:], 7)
+        put_hi(PACK - 1)
+
+        def y_pass(acc, a, tp, x_codes, x_plane):
+            for n in range(2):
+                t = 2 * tp + n
+                nc.tensor.matmul_mx(
+                    out=acc[:, n, :],
+                    lhsT=w4_codes[:, a, t, :].bitcast(FP8X4), lhsT_scale=w4_dealt[:, a, t, :],
+                    rhs=x_codes.bitcast(FP8X4), rhs_scale=x_plane,
+                    start=(a == 0 and n == 0), stop=(a == PASSES - 1 and n == 1),
+                )
+
+        y_banks = {}
+        for hf in range(2):
+            cols = slice(HALF_M * hf, HALF_M * (hf + 1))
+            for tp in range(2):
+                acc = bank(f"y_{hf}{tp}", ("bank_c", "bank_b")[hf], [P, 2, HALF_M])
+                y_pass(acc, 0, tp, x0_codes[:, cols], x0_plane[:, cols])
+                y_banks[hf, tp] = acc
+
+        for hf in range(2):
+            cols = slice(HALF_M * hf, HALF_M * (hf + 1))
+            fetch_difference(x_hi[:, PACK - 1, cols], 7, before7[:, cols], slice(16 * hf, 16 * (hf + 1)))
+
+        y_rows = out_0.rearrange("(p t) m -> p t m", t=PACK)
+        y_plane = sb("y_plane", [P, M], U8)
+        for hf in range(2):
+            cols = slice(HALF_M * hf, HALF_M * (hf + 1))
+            x_bf = sb(f"x1_bf{hf}", [P, PACK * HALF_M], BF16)
+            interleave((nc.scalar.copy, nc.vector.tensor_copy)[hf], x_bf[:], x_hi[:, :, cols])
+            x_codes = sb(f"x1_codes{hf}", [P, HALF_M], U32)
+            x_plane = sb(f"x1_plane{hf}", [P, HALF_M], U8)
+            nc.vector.quantize_mx(out=x_codes[:].bitcast(FP8X4), scales=x_plane[:], in_=x_bf[:])
+            y = sb(f"y{hf}", [P, PACK, HALF_M], F32, tag=f"raw3_1{hf}")
+            for tp in range(2):
+                acc = y_banks[hf, tp]
+                y_pass(acc, 1, tp, x_codes[:], x_plane[:])
+                for n in range(2):
+                    t = 2 * tp + n
+                    if tp == 0:
+                        nc.scalar.activation(y[:, t, :], acc[:, n, :], ACT.Identity, bias=b4_dealt[:, t : t + 1])
+                    else:
+                        nc.vector.tensor_scalar(y[:, t, :], acc[:, n, :], b4_dealt[:, t : t + 1], None, ALU.add)
+            nc.sync.dma_start(out=y_rows[:, :, cols], in_=y[:])
+            y_bf = sb(f"y_bf{hf}", [P, PACK * HALF_M], BF16)
+            interleave(nc.vector.tensor_copy, y_bf[:], y[:])
+            y_codes = sb(f"y_codes{hf}", [P, HALF_M], I32)
+            nc.vector.quantize_mx(out=y_codes[:].bitcast(FP8X4), scales=y_plane[:, cols], in_=y_bf[:])
+            nc.scalar.dma_start(
+                out=out_1[0, :, cols, :].rearrange("p m t -> p (m t)").bitcast(I32), in_=y_codes[:]
+            )
+        for q in range(P // QUAD):
+            (nc.sync, nc.scalar)[q % 2].dma_start(
+                out=out_2[0, 4 * q : 4 * q + 4, :].bitcast(I32),
+                in_=y_plane[QUAD * q : QUAD * q + 4, :].bitcast(I32),
+            )

@@ -57,14 +57,14 @@ def tile_list_waterhole_redistribution_features_kernel(
             nc.sync.dma_start(out=t[:], in_=rows)
             return t
 
-        def zero_plane(engine, name, width):
-            plane = sb(name, [P, PASSES, width], U8)
-            engine.memset(plane[:].bitcast(I32), 0)
+        def zero_plane(name, width, tag=None):
+            plane = sb(name, [P, PASSES, width], U8, tag=tag)
+            nc.vector.memset(plane[:].bitcast(I32), 0)
             return plane
 
-        def load_scales(queue, plane, src):
+        def load_scales(plane, src):
             for q in range(P // QUAD):
-                queue.dma_start(
+                nc.gpsimd.dma_start(
                     out=plane[QUAD * q : QUAD * q + 4, :, :].bitcast(I32),
                     in_=src[:, 4 * q : 4 * q + 4, :].rearrange("a r c -> r a c").bitcast(I32),
                 )
@@ -75,14 +75,13 @@ def tile_list_waterhole_redistribution_features_kernel(
                 in_=src.rearrange("p t (c i) -> p c t i", i=4),
             )
 
-        tab_plane = zero_plane(nc.gpsimd, "tab_plane", T)
-        w3_plane = zero_plane(nc.vector, "w3_plane", H)
-        w4_plane = zero_plane(nc.vector, "w4_plane", N)
-        load_scales(nc.scalar, tab_plane, tab_scales)
-        load_scales(nc.gpsimd, w3_plane, w3_scales)
         gain_nat = sb("gain_nat", [P, PACK], F32)
         with nc.allow_non_contiguous_dma(reason="one gain a partition"):
             nc.gpsimd.dma_start(out=gain_nat[:], in_=gain[0:KP].rearrange("(b p) -> p b", p=P))
+        tab_plane = zero_plane("tab_plane", T)
+        w3_plane = zero_plane("w3_plane", H)
+        load_scales(tab_plane, tab_scales)
+        load_scales(w3_plane, w3_scales)
 
         def load_table(a):
             t = sb(f"tabw{a}", [P, T], I32)
@@ -91,31 +90,40 @@ def tile_list_waterhole_redistribution_features_kernel(
 
         raw = {}
 
-        def load_chunk(c, which, col0, width):
-            for wi in which:
-                for a in range(PASSES):
-                    raw[c, wi, a] = load_weight_piece(f"raw{c}_{wi}{a}", (w1, w2)[wi], a, col0, width)
+        W1, W2 = [(0, 0), (0, 1)], [(1, 0), (1, 1)]
+
+        def load_chunk(c, pieces, col0, width):
+            for wi, a in pieces:
+                raw[c, wi, a] = load_weight_piece(f"raw{c}_{wi}{a}", (w1, w2)[wi], a, col0, width)
+
+        def load_w3(name, col0):
+            t = sb(name, [P, PASSES, 2 * KP], U8)
+            src = w3_words[:, :, 2 * col0 : 2 * (col0 + KP)].rearrange("a p c -> p a c")
+            nc.sync.dma_start(out=t[:].bitcast(I32), in_=src.bitcast(I32))
+            return t
 
         idx = load_list("idx", offs)
-        load_chunk(0, (0,), 0, P)
+        load_chunk(0, W1, 0, P)
         tabw = [load_table(0)]
-        load_chunk(0, (1,), 0, P)
+        load_chunk(0, W2, 0, P)
         tabw.append(load_table(1))
-        w3_codes = sb("w3_codes", [P, PASSES, 2 * H], U8)
-        nc.sync.dma_start(out=w3_codes[:].bitcast(I32), in_=w3_words.rearrange("a p c -> p a c").bitcast(I32))
+        w3_codes = [load_w3("w3_lo", 0)]
         page = [load_page("page0", page0[0:P, :])]
         wgs_nat = sb("wgs_nat", [P, S], F32)
         nc.sync.dma_start(out=wgs_nat[:], in_=wgs)
         idx4 = load_list("idx4", offs4)
         idx2 = load_list("idx2", offs2)
-        load_chunk(1, (0, 1), P, P)
+        load_chunk(1, W1 + W2, P, P)
         idx3 = load_list("idx3", offs3)
+        w3_codes.append(load_w3("w3_hi", KP))
+        w4_raw = sb("w4_raw", [P, PASSES, N], I32)
+        nc.sync.dma_start(out=w4_raw[:], in_=w4_words.rearrange("a p c i -> p a (c i)").bitcast(I32))
         page.append(load_page("page1", page0[P : 2 * P, :]))
-        load_chunk(2, (0, 1), 2 * P, 2 * P)
+        load_chunk(2, W1 + W2, 2 * P, 2 * P)
         page.append(load_page("page2", page0[2 * P : 3 * P, :]))
-        load_chunk(3, (0,), KP, KP)
+        load_chunk(3, W1[:1], KP, KP)
         page.append(load_page("page3", page0[3 * P : 4 * P, :]))
-        load_chunk(3, (1,), KP, KP)
+        load_chunk(3, W1[1:] + W2, KP, KP)
         page_hi = page0[KP:H, :].rearrange("(p t) c -> p t c", t=PACK)
         page.append(load_page("page4", page_hi[:, 0, :]))
         wgs_dealt = sb("wgs_dealt", [P, PACK, S], F32)
@@ -128,9 +136,6 @@ def tile_list_waterhole_redistribution_features_kernel(
             page.append(load_page(f"page{4 + t}", page_hi[:, t, :]))
         gain_dealt = sb("gain_dealt", [P, PACK], F32)
         nc.sync.dma_start(out=gain_dealt[:], in_=gain[KP:H].rearrange("(p t) -> p t", t=PACK))
-        w4_raw = sb("w4_raw", [P, PASSES, N], I32)
-        nc.sync.dma_start(out=w4_raw[:], in_=w4_words.rearrange("a p c i -> p a (c i)").bitcast(I32))
-        load_scales(nc.sync, w4_plane, w4_scales)
         b4_dealt = sb("b4_dealt", [P, PACK], F32)
         nc.sync.dma_start(out=b4_dealt[:], in_=b4.rearrange("(p t) -> p t", t=PACK))
 
@@ -146,25 +151,21 @@ def tile_list_waterhole_redistribution_features_kernel(
             vw.append(w_t)
             vs.append(s_t)
 
-        codes, planes = {}, {}
+        operands = {}
 
-        def new_operands(c, which, width, tag):
-            words = sb(f"codes{c}_{which[0]}", [P, len(which), PASSES, width], U32, tag=tag)
-            plane = sb(f"planes{c}_{which[0]}", [P, len(which), PASSES, width], U8)
-            flat = "p w a c -> p (w a c)"
-            for n, wi in enumerate(which):
-                for a in range(PASSES):
-                    start = (PASSES * n + a) * width
-                    codes[c, wi, a] = (words[:].rearrange(flat), start)
-                    planes[c, wi, a] = (plane[:].rearrange(flat), start)
+        def new_operands(c, pieces, width, tag):
+            name = f"{c}_{pieces[0][0]}{pieces[0][1]}"
+            words = sb(f"codes{name}", [P, len(pieces) * width], U32, tag=tag)
+            plane = sb(f"plane{name}", [P, len(pieces) * width], U8)
+            for n, piece in enumerate(pieces):
+                operands[(c,) + piece] = (words, plane, n * width)
 
-        def quantise(c, width, pieces):
-            tag = f"stage{c}_{pieces[0][0]}{pieces[0][1]}"
-            stage = sb(tag, [P, len(pieces), PACK * width], BF16)
+        def quantise(c, pieces, width, tag=None):
+            tag = tag or f"stage{c}_{pieces[0][0]}{pieces[0][1]}"
+            stage = sb(f"stage{c}_{pieces[0][0]}{pieces[0][1]}", [P, len(pieces), PACK * width], BF16, tag=tag)
             for n, (wi, a) in enumerate(pieces):
                 interleave(nc.scalar.copy, stage[:, n, :], raw[c, wi, a][:])
-            words, start = codes[(c,) + pieces[0]]
-            plane, start = planes[(c,) + pieces[0]]
+            words, plane, start = operands[(c,) + pieces[0]]
             span = slice(start, start + len(pieces) * width)
             nc.vector.quantize_mx(
                 out=words[:, span].bitcast(FP8X4), scales=plane[:, span], in_=stage[:].rearrange("p n c -> p (n c)")
@@ -183,172 +184,188 @@ def tile_list_waterhole_redistribution_features_kernel(
         def table(cols):
             return lambda a: (vw[a][:, cols].bitcast(FP8X4), vs[a][:, cols])
 
-        def weight(c, wi, cols):
+        def weight(c, wi, width):
             def operand(a):
-                words, start = codes[c, wi, a]
-                plane, start = planes[c, wi, a]
-                span = slice(start + cols.start, start + cols.stop)
-                return words[:, span].bitcast(FP8X4), plane[:, span]
+                words, plane, start = operands[c, wi, a]
+                return words[:, start : start + width].bitcast(FP8X4), plane[:, start : start + width]
 
             return operand
 
         def weight3(col0, width):
             return lambda a: (
-                w3_codes[:, a, 2 * col0 : 2 * (col0 + width)].bitcast(FP4X4),
+                w3_codes[col0 // KP][:, a, 2 * (col0 % KP) : 2 * (col0 % KP + width)].bitcast(FP4X4),
                 w3_plane[:, a, col0 : col0 + width],
             )
 
-        everything = slice(0, S)
-
-        h_lo = {}
-
-        def products_lo(b, c, col0):
-            cols = slice(col0, col0 + P)
-            h1 = bank(f"h1_{b}", "bank_a", [P, S])
-            product(h1[:], weight(c, 0, cols), table(everything))
-            h3 = bank(f"h3_{b}", "bank_c", [P, S])
-            product(h3[:], weight3(P * b, P), table(everything))
-            h2 = bank(f"h2_{b}", "bank_b", [P, S])
-            product(h2[:], weight(c, 1, cols), table(everything))
-            rec = sb(f"rec{b}", [P, S], F32)
-            nc.scalar.activation(rec[:], h1[:], ACT.Tanh)
-            wg = sb(f"wg{b}", [P, S], F32)
-            nc.scalar.activation(wg[:], wgs_nat[:], ACT.Copy, scale=gain_nat[:, b : b + 1])
-            h_lo[b] = (rec, h2, h3, wg)
-
-        def put_lo(b):
-            rec, h2, h3, wg = h_lo[b]
-            nc.vector.tensor_tensor(rec[:], rec[:], h2[:], ALU.max)
-            nc.vector.tensor_tensor(rec[:], rec[:], h3[:], ALU.add)
-            nc.vector.tensor_tensor(page[b][:].indirect(idx2[:]), rec[:], wg[:], ALU.mult)
-
         def fetch_before(dst, b):
             nc.vector.tensor_copy(dst, page[b][:].indirect(idx4[:]))
+            before[b] = dst
 
-        def fetch_difference(dst, b, before, lists_cols):
-            nc.vector.tensor_tensor(dst, page[b][:].indirect(idx3[:, lists_cols]), before, ALU.subtract)
+        def fetch_difference(dst, b, cols):
+            picks = idx3[:, cols.start // 16 : cols.stop // 16]
+            nc.vector.tensor_tensor(dst, page[b][:].indirect(picks), before[b][:, cols], ALU.subtract)
 
-        all_cols = slice(0, M // 16)
+        def put(b, records, weights):
+            nc.vector.tensor_tensor(page[b][:].indirect(idx2[:]), records, weights, ALU.mult)
 
-        new_operands(0, (0, 1), P, None)
-        for wi in range(2):
-            for a in range(PASSES):
-                quantise(0, P, [(wi, a)])
-        products_lo(0, 0, 0)
+        before = {}
+        x_lo = {}
+        whole = slice(0, S)
+
+        def direct_products(b, tanh_tag):
+            h1 = bank(f"h1_{b}", "bank_a", [P, S])
+            product(h1[:], weight(b, 0, P), table(whole))
+            h2 = bank(f"h2_{b}", "bank_b", [P, S])
+            product(h2[:], weight(b, 1, P), table(whole))
+            h3 = bank(f"h3_{b}", "bank_c", [P, S])
+            product(h3[:], weight3(P * b, P), table(whole))
+            th = sb(f"tanh{b}", [P, S], F32, tag=tanh_tag)
+            nc.scalar.activation(th[:], h1[:], ACT.Tanh)
+            wg = sb(f"wg{b}", [P, S], F32)
+            nc.scalar.activation(wg[:], wgs_nat[:], ACT.Copy, scale=gain_nat[:, b : b + 1])
+            return th, h2, h3, wg
+
+        def direct_put(b, th, h2, h3, wg):
+            rec = sb(f"rec{b}", [P, S], F32)
+            nc.vector.tensor_tensor(rec[:], th[:], h2[:], ALU.max)
+            nc.vector.tensor_tensor(rec[:], rec[:], h3[:], ALU.add)
+            put(b, rec[:], wg[:])
+
+        def turned(name, bank_tags, tile_tags, moving, width, finish):
+            per_bank = KP // width
+            tiles = []
+            for n, tile_tag in enumerate(tile_tags):
+                acc = bank(f"{name}_acc{n}", bank_tags[n % len(bank_tags)], [P, KP])
+                for m in range(per_bank):
+                    jb = per_bank * n + m
+                    product(acc[:, width * m : width * (m + 1)], table(slice(P * jb, P * (jb + 1))), moving)
+                dst = sb(f"{name}{n}", [P, KP], F32, tag=tile_tag)
+                if per_bank == 1:
+                    finish(n, dst[:].rearrange("p (t q) -> p t q", t=PACK), acc[:].rearrange("p (q t) -> p t q", t=PACK))
+                else:
+                    finish(n, dst[:], acc[:])
+                tiles.append(dst)
+            return tiles
+
+        def copy_out(n, dst, acc):
+            nc.scalar.copy(out=dst, in_=acc)
+
+        def tanh_out(n, dst, acc):
+            nc.scalar.activation(dst, acc, ACT.Tanh)
+
+        def max_with(tanh_tiles):
+            def finish(n, dst, acc):
+                th = tanh_tiles[n][:]
+                if len(dst.shape) == 3:
+                    th = th.rearrange("p (t q) -> p t q", t=PACK)
+                nc.vector.tensor_tensor(dst, th, acc, ALU.max)
+
+            return finish
+
+        def turn_back(b, s, width, terms, gain_col, tag):
+            per_bank = KP // width
+            acc = bank(f"sum{b}", "bank_s", [P, S])
+            steps = [(tiles, jb) for tiles in terms for jb in range(S // P)]
+            for n, (tiles, jb) in enumerate(steps):
+                col0 = (jb % per_bank) * width + P * s
+                nc.tensor.matmul(
+                    acc[:, P * jb : P * (jb + 1)], tiles[jb // per_bank][:, col0 : col0 + P], ident[:],
+                    start=(n == 0), stop=(n == len(steps) - 1), is_transpose=True,
+                )
+            rec = sb(f"rec{b}", [P, S], F32, tag=tag)
+            nc.scalar.activation(rec[:], acc[:], ACT.Copy, scale=gain_col)
+            return rec
+
+        def close_slice(b, tag):
+            pair = sb(f"pair{b}", [P, 2, M], F32, tag=tag)
+            fetch_difference(pair[:, 0, :], b, whole)
+            fetch_before(pair[:, 1, :], b + 1)
+            x_lo[b] = pair[:, 0, :]
+
+        new_operands(0, W1 + W2, P, None)
+        for piece in W1 + W2:
+            quantise(0, [piece], P)
+        parts = direct_products(0, "tanh0")
         before0 = sb("before0", [P, M], F32)
         fetch_before(before0[:], 0)
-        before = {0: before0[:]}
-        put_lo(0)
+        direct_put(0, *parts)
 
-        h3_hi = []
-        for jb in range(S // P):
-            acc = bank(f"h3t_{jb}", "bank_s", [P, KP])
-            product(acc[:], table(slice(P * jb, P * (jb + 1))), weight3(KP, KP))
-            c3 = sb(f"h3_hi{jb}", [P, PACK, P], F32, tag=f"raw0_{jb // 2}{jb % 2}")
-            nc.scalar.copy(out=c3[:], in_=acc[:].rearrange("p (q t) -> p t q", t=PACK))
-            h3_hi.append(c3)
+        w4_plane = zero_plane("w4_plane", N, tag="stage0_11")
+        load_scales(w4_plane, w4_scales)
 
-        x_lo = {}
-
-        def close_lo(b, tag):
-            pair = sb(f"pair{b}", [P, 2, M], F32, tag=tag)
-            fetch_difference(pair[:, 0, :], b, before[b], all_cols)
-            fetch_before(pair[:, 1, :], b + 1)
-            before[b + 1] = pair[:, 1, :]
-            x_lo[b] = pair
-
-        new_operands(1, (0, 1), P, "wg0")
-        tag = quantise(1, P, [(0, 0), (0, 1), (1, 0), (1, 1)])
-        products_lo(1, 1, 0)
-        close_lo(0, tag)
-        put_lo(1)
-
-        new_operands(2, (0, 1), 2 * P, "wg1")
-        quantise(2, 2 * P, [(0, 0), (0, 1)])
-        tag = quantise(2, 2 * P, [(1, 0), (1, 1)])
-        products_lo(2, 2, 0)
-        products_lo(3, 2, P)
-        close_lo(1, tag)
-        put_lo(2)
-
-        new_operands(3, (0,), KP, "wg2")
-        quantise(3, KP, [(0, 0)])
-        tag = quantise(3, KP, [(0, 1)])
-        tanh_tags = ["raw1_00", "raw1_01", "raw1_10", "raw2_00"]
-        tanh_hi = []
-        for jb in range(S // P):
-            acc = bank(f"h1t_{jb}", "bank_a", [P, KP])
-            product(acc[:], table(slice(P * jb, P * (jb + 1))), weight(3, 0, slice(0, KP)))
-            th = sb(f"tanh_hi{jb}", [P, PACK, P], F32, tag=tanh_tags[jb])
-            nc.scalar.activation(th[:], acc[:].rearrange("p (q t) -> p t q", t=PACK), ACT.Tanh)
-            tanh_hi.append(th)
-        close_lo(2, tag)
-        put_lo(3)
-
-        new_operands(3, (1,), KP, "wg3")
-        quantise(3, KP, [(1, 0)])
-        tag = quantise(3, KP, [(1, 1)])
-        close_lo(3, tag)
-        max_tags = ["raw1_11", "raw2_01", "raw2_10", "raw2_11"]
-        max_hi = []
-        for jb in range(S // P):
-            acc = bank(f"h2t_{jb}", ("bank_b", "bank_a")[jb % 2], [P, KP])
-            product(acc[:], table(slice(P * jb, P * (jb + 1))), weight(3, 1, slice(0, KP)))
-            mx = sb(f"max_hi{jb}", [P, PACK, P], F32, tag=max_tags[jb])
-            nc.vector.tensor_tensor(mx[:], tanh_hi[jb][:], acc[:].rearrange("p (q t) -> p t q", t=PACK), ALU.max)
-            max_hi.append(mx)
-
-        rec_hi = []
-        for t in range(PACK):
-            acc = bank(f"sum_{t}", "bank_s", [P, S])
-            terms = [(src, jb) for src in (h3_hi, max_hi) for jb in range(S // P)]
-            for n, (src, jb) in enumerate(terms):
-                nc.tensor.matmul(
-                    acc[:, P * jb : P * (jb + 1)], src[jb][:, t, :], ident[:],
-                    start=(n == 0), stop=(n == len(terms) - 1), is_transpose=True,
-                )
-            rec = sb(f"rec_hi{t}", [P, S], F32, tag=f"rec{t}")
-            nc.scalar.activation(rec[:], acc[:], ACT.Copy, scale=gain_dealt[:, t : t + 1])
-            rec_hi.append(rec)
-
-        pair56 = sb("pair56", [P, 2, M], F32, tag=tanh_tags[3])
-        for n in range(2):
-            fetch_before(pair56[:, n, :], 5 + n)
-            before[5 + n] = pair56[:, n, :]
-
-        w4_codes = sb("w4_codes", [P, PASSES, PACK, P], I32)
+        new_operands(1, W1 + W2, P, "wg0")
+        quantise(1, W1, P, tag="tanh0")
+        tag = quantise(1, W2, P)
+        parts = direct_products(1, None)
+        close_slice(0, tag)
+        w4_codes = sb("w4_codes", [P, PASSES, PACK, P], I32, tag="tanh0")
         nc.vector.tensor_copy(
             out=w4_codes[:].rearrange("p a t q -> p a q t"),
             in_=w4_raw[:].rearrange("p a (q t) -> p a q t", t=PACK),
         )
-        w4_dealt = sb("w4_dealt", [P, PASSES, PACK, P], U8)
+        direct_put(1, *parts)
+
+        h3_mid = turned("h3_mid", ["bank_s"], ["stage0_00", "before0"], weight3(2 * P, 2 * P), 2 * P, copy_out)
+        h3_hi = turned("h3_hi", ["bank_s"], ["raw0_00", "raw0_01", "raw0_10", "raw0_11"], weight3(KP, KP), KP, copy_out)
+
+        new_operands(2, W1 + W2, 2 * P, "wg1")
+        tag_w1 = quantise(2, W1, 2 * P)
+        tag = quantise(2, W2, 2 * P)
+        tanh_mid = turned("tanh_mid", ["bank_a"], ["tanh_mid0", "tanh_mid1"], weight(2, 0, 2 * P), 2 * P, tanh_out)
+        close_slice(1, tag)
+        w4_dealt = sb("w4_dealt", [P, PASSES, PACK, P], U8, tag=tag_w1)
         nc.vector.tensor_copy(
             out=w4_dealt[:].rearrange("p a t q -> p a q t"),
             in_=w4_plane[:].rearrange("p a (q t) -> p a q t", t=PACK),
         )
+        max_mid = turned("max_mid", ["bank_b"], ["wg0", "codes0_00"], weight(2, 1, 2 * P), 2 * P, max_with(tanh_mid))
+        rec = {b: turn_back(b, b - 2, 2 * P, (h3_mid, max_mid), gain_nat[:, b : b + 1], None) for b in (2, 3)}
+        before3 = sb("before3", [P, M], F32, tag="tanh_mid1")
+        fetch_before(before3[:], 3)
+        new_operands(3, W1[:1], KP, "tanh_mid0")
+        quantise(3, W1[:1], KP)
+        put(2, rec[2][:], wgs_nat[:])
+        new_operands(3, W1[1:], KP, "rec2")
+        tag = quantise(3, W1[1:], KP)
+        tanh_tags = ["raw1_00", "raw1_01", "raw1_10", "raw2_00"]
+        tanh_hi = turned("tanh_hi", ["bank_a"], tanh_tags, weight(3, 0, KP), KP, tanh_out)
+        x2 = sb("x2", [P, M], F32, tag=tag)
+        fetch_difference(x2[:], 2, whole)
+        x_lo[2] = x2[:]
+        put(3, rec[3][:], wgs_nat[:])
 
-        x_hi = sb("x_hi", [P, PACK, M], F32, tag="raw3_01")
-
-        def put_hi(t):
-            nc.vector.tensor_tensor(page[4 + t][:].indirect(idx2[:]), rec_hi[t][:], wgs_dealt[:, t, :], ALU.mult)
-
-        for t in range(PACK - 1):
-            put_hi(t)
-            fetch_difference(x_hi[:, t, :], 4 + t, before[4 + t], all_cols)
+        new_operands(3, W2, KP, "rec3")
+        quantise(3, W2[:1], KP)
+        tag = quantise(3, W2[1:], KP)
+        close_slice(3, tag)
+        max_tags = ["raw1_11", "raw2_01", "raw2_10", "raw2_11"]
+        max_hi = turned("max_hi", ["bank_b", "bank_a"], max_tags, weight(3, 1, KP), KP, max_with(tanh_hi))
 
         x_moved = sb("x_moved", [P, PACK, M], F32, tag="raw3_00")
         for b in range(PACK):
             for t in range(PACK):
-                nc.sync.dma_start(out=x_moved[QUAD * b : QUAD * (b + 1), t, :], in_=x_lo[b][t:P:PACK, 0, :])
-        x0_bf = sb("x0_bf", [P, PACK * M], BF16, tag=max_tags[3])
+                nc.sync.dma_start(out=x_moved[QUAD * b : QUAD * (b + 1), t, :], in_=x_lo[b][t:P:PACK, :])
+
+        rec_tags = ["rec0", "rec1", "rec2", "raw3_00"]
+        for t in range(PACK - 1):
+            rec[4 + t] = turn_back(4 + t, t, KP, (h3_hi, max_hi), gain_dealt[:, t : t + 1], rec_tags[t])
+        x0_bf = sb("x0_bf", [P, PACK * M], BF16, tag="stage3_00")
         interleave(nc.scalar.copy, x0_bf[:], x_moved[:])
-        x0_codes = sb("x0_codes", [P, M], U32)
+        rec[7] = turn_back(7, 3, KP, (h3_hi, max_hi), gain_dealt[:, 3:4], rec_tags[3])
+
+        before_hi = sb("before_hi", [P, PACK - 1, M], F32, tag=tanh_tags[3])
+        for n in range(PACK - 1):
+            fetch_before(before_hi[:, n, :], 5 + n)
+
+        x_hi = sb("x_hi", [P, PACK, M], F32, tag="raw3_01")
+        put(4, rec[4][:], wgs_dealt[:, 0, :])
+        for t in range(PACK - 1):
+            put(5 + t, rec[5 + t][:], wgs_dealt[:, t + 1, :])
+            fetch_difference(x_hi[:, t, :], 4 + t, whole)
+
+        x0_codes = sb("x0_codes", [P, M], U32, tag=rec_tags[3])
         x0_plane = sb("x0_plane", [P, M], U8)
         nc.vector.quantize_mx(out=x0_codes[:].bitcast(FP8X4), scales=x0_plane[:], in_=x0_bf[:])
-
-        before7 = sb("before7", [P, M], F32, tag=max_tags[3])
-        fetch_before(before7[:], 7)
-        put_hi(PACK - 1)
 
         def y_pass(acc, a, tp, x_codes, x_plane):
             for n in range(2):
@@ -370,7 +387,7 @@ def tile_list_waterhole_redistribution_features_kernel(
 
         for hf in range(2):
             cols = slice(HALF_M * hf, HALF_M * (hf + 1))
-            fetch_difference(x_hi[:, PACK - 1, cols], 7, before7[:, cols], slice(16 * hf, 16 * (hf + 1)))
+            fetch_difference(x_hi[:, PACK - 1, cols], 7, cols)
 
         y_rows = out_0.rearrange("(p t) m -> p t m", t=PACK)
         y_plane = sb("y_plane", [P, M], U8)

@@ -71,8 +71,8 @@ def tile_list_waterhole_redistribution_features_kernel(
 
         def interleave(engine_copy, dst, src):
             engine_copy(
-                out=dst.rearrange("p (c i t) -> p c t i", i=4, t=PACK),
-                in_=src.rearrange("p t (c i) -> p c t i", i=4),
+                out=dst.rearrange("p (c t) -> p c t", t=PACK),
+                in_=src.rearrange("p t c -> p c t"),
             )
 
         gain_nat = sb("gain_nat", [P, PACK], F32)
@@ -315,8 +315,8 @@ def tile_list_waterhole_redistribution_features_kernel(
         close_slice(1, tag)
         w4_dealt = sb("w4_dealt", [P, PASSES, PACK, P], U8, tag=tag_w1)
         nc.vector.tensor_copy(
-            out=w4_dealt[:].rearrange("p a t q -> p a q t"),
-            in_=w4_plane[:].rearrange("p a (q t) -> p a q t", t=PACK),
+            out=w4_dealt[:],
+            in_=w4_plane[:].rearrange("p a (q t) -> p a t q", t=PACK),
         )
         max_mid = turned("max_mid", ["bank_b"], ["wg0", "codes0_00"], weight(2, 1, 2 * P), 2 * P, max_with(tanh_mid))
         rec = {b: turn_back(b, b - 2, 2 * P, (h3_mid, max_mid), gain_nat[:, b : b + 1], None) for b in (2, 3)}

@@ -57,31 +57,31 @@ def tile_list_waterhole_redistribution_features_kernel(
             nc.sync.dma_start(out=t[:], in_=rows)
             return t
 
-        def zero_plane(name, width, tag=None):
+        def zero_plane(engine, name, width, tag=None):
             plane = sb(name, [P, PASSES, width], U8, tag=tag)
-            nc.vector.memset(plane[:].bitcast(I32), 0)
+            engine.memset(plane[:].bitcast(I32), 0)
             return plane
 
-        def load_scales(plane, src):
+        def load_scales(queue, plane, src):
             for q in range(P // QUAD):
-                nc.gpsimd.dma_start(
+                queue.dma_start(
                     out=plane[QUAD * q : QUAD * q + 4, :, :].bitcast(I32),
                     in_=src[:, 4 * q : 4 * q + 4, :].rearrange("a r c -> r a c").bitcast(I32),
                 )
 
         def interleave(engine_copy, dst, src):
             engine_copy(
-                out=dst.rearrange("p (c t) -> p c t", t=PACK),
-                in_=src.rearrange("p t c -> p c t"),
+                out=dst.rearrange("p (c i t) -> p c t i", i=4, t=PACK),
+                in_=src.rearrange("p t (c i) -> p c t i", i=4),
             )
 
-        gain_nat = sb("gain_nat", [P, PACK], F32)
-        with nc.allow_non_contiguous_dma(reason="one gain a partition"):
-            nc.gpsimd.dma_start(out=gain_nat[:], in_=gain[0:KP].rearrange("(b p) -> p b", p=P))
-        tab_plane = zero_plane("tab_plane", T)
-        w3_plane = zero_plane("w3_plane", H)
-        load_scales(tab_plane, tab_scales)
-        load_scales(w3_plane, w3_scales)
+        tab_plane = zero_plane(nc.gpsimd, "tab_plane", T)
+        w3_plane = zero_plane(nc.vector, "w3_plane", H)
+        gain_rows = sb("gain_rows", [P, P], F32)
+        nc.gpsimd.memset(gain_rows[:], 0.0)
+        nc.gpsimd.dma_start(out=gain_rows[0:PACK, :], in_=gain[0:KP].rearrange("(b p) -> b p", p=P))
+        load_scales(nc.scalar, tab_plane, tab_scales)
+        load_scales(nc.gpsimd, w3_plane, w3_scales)
 
         def load_table(a):
             t = sb(f"tabw{a}", [P, T], I32)
@@ -108,22 +108,22 @@ def tile_list_waterhole_redistribution_features_kernel(
         load_chunk(0, W2, 0, P)
         tabw.append(load_table(1))
         w3_codes = [load_w3("w3_lo", 0)]
+        idx4 = load_list("idx4", offs4)
         page = [load_page("page0", page0[0:P, :])]
         wgs_nat = sb("wgs_nat", [P, S], F32)
         nc.sync.dma_start(out=wgs_nat[:], in_=wgs)
-        idx4 = load_list("idx4", offs4)
         idx2 = load_list("idx2", offs2)
         load_chunk(1, W1 + W2, P, P)
         idx3 = load_list("idx3", offs3)
-        w3_codes.append(load_w3("w3_hi", KP))
-        w4_raw = sb("w4_raw", [P, PASSES, N], I32)
-        nc.sync.dma_start(out=w4_raw[:], in_=w4_words.rearrange("a p c i -> p a (c i)").bitcast(I32))
         page.append(load_page("page1", page0[P : 2 * P, :]))
         load_chunk(2, W1 + W2, 2 * P, 2 * P)
         page.append(load_page("page2", page0[2 * P : 3 * P, :]))
         load_chunk(3, W1[:1], KP, KP)
         page.append(load_page("page3", page0[3 * P : 4 * P, :]))
         load_chunk(3, W1[1:] + W2, KP, KP)
+        w3_codes.append(load_w3("w3_hi", KP))
+        w4_raw = sb("w4_raw", [P, PASSES, N], I32)
+        nc.sync.dma_start(out=w4_raw[:], in_=w4_words.rearrange("a p c i -> p a (c i)").bitcast(I32))
         page_hi = page0[KP:H, :].rearrange("(p t) c -> p t c", t=PACK)
         page.append(load_page("page4", page_hi[:, 0, :]))
         wgs_dealt = sb("wgs_dealt", [P, PACK, S], F32)
@@ -141,6 +141,10 @@ def tile_list_waterhole_redistribution_features_kernel(
 
         ident = sb("ident", [P, P], F32)
         make_identity(nc, ident[:])
+        gain_turned = bank("gain_turned", "bank_s", [P, P])
+        nc.tensor.transpose(gain_turned[:], gain_rows[:], ident[:])
+        gain_nat = sb("gain_nat", [P, PACK], F32)
+        nc.scalar.copy(out=gain_nat[:], in_=gain_turned[:, 0:PACK])
 
         vw, vs = [], []
         for a in range(PASSES):
@@ -227,8 +231,9 @@ def tile_list_waterhole_redistribution_features_kernel(
 
         def direct_put(b, th, h2, h3, wg):
             rec = sb(f"rec{b}", [P, S], F32)
-            nc.vector.tensor_tensor(rec[:], th[:], h2[:], ALU.max)
-            nc.vector.tensor_tensor(rec[:], rec[:], h3[:], ALU.add)
+            larger = sb(f"larger{b}", [P, S], F32)
+            nc.vector.tensor_tensor(larger[:], th[:], h2[:], ALU.max)
+            nc.vector.tensor_tensor(rec[:], larger[:], h3[:], ALU.add)
             put(b, rec[:], wg[:])
 
         def turned(name, bank_tags, tile_tags, moving, width, finish):
@@ -290,53 +295,42 @@ def tile_list_waterhole_redistribution_features_kernel(
         fetch_before(before0[:], 0)
         direct_put(0, *parts)
 
-        w4_plane = zero_plane("w4_plane", N, tag="stage0_11")
-        load_scales(w4_plane, w4_scales)
+        w4_plane = zero_plane(nc.vector, "w4_plane", N, tag="stage0_11")
+        load_scales(nc.gpsimd, w4_plane, w4_scales)
 
-        new_operands(1, W1 + W2, P, "wg0")
+        new_operands(1, W1 + W2, P, "larger0")
         quantise(1, W1, P, tag="tanh0")
         tag = quantise(1, W2, P)
         parts = direct_products(1, None)
         close_slice(0, tag)
-        w4_codes = sb("w4_codes", [P, PASSES, PACK, P], I32, tag="tanh0")
-        nc.vector.tensor_copy(
-            out=w4_codes[:].rearrange("p a t q -> p a q t"),
-            in_=w4_raw[:].rearrange("p a (q t) -> p a q t", t=PACK),
-        )
         direct_put(1, *parts)
 
-        h3_mid = turned("h3_mid", ["bank_s"], ["stage0_00", "before0"], weight3(2 * P, 2 * P), 2 * P, copy_out)
-        h3_hi = turned("h3_hi", ["bank_s"], ["raw0_00", "raw0_01", "raw0_10", "raw0_11"], weight3(KP, KP), KP, copy_out)
+        h3_mid = turned("h3_mid", ["bank_s"], ["stage0_00", "stage0_01"], weight3(2 * P, 2 * P), 2 * P, copy_out)
 
-        new_operands(2, W1 + W2, 2 * P, "wg1")
-        tag_w1 = quantise(2, W1, 2 * P)
-        tag = quantise(2, W2, 2 * P)
+        new_operands(2, W1 + W2, 2 * P, "larger1")
+        tag_w1 = quantise(2, W1, 2 * P, tag="before0")
+        tag = quantise(2, W2, 2 * P, tag="tanh1")
         tanh_mid = turned("tanh_mid", ["bank_a"], ["tanh_mid0", "tanh_mid1"], weight(2, 0, 2 * P), 2 * P, tanh_out)
         close_slice(1, tag)
-        w4_dealt = sb("w4_dealt", [P, PASSES, PACK, P], U8, tag=tag_w1)
-        nc.vector.tensor_copy(
-            out=w4_dealt[:],
-            in_=w4_plane[:].rearrange("p a (q t) -> p a t q", t=PACK),
-        )
         max_mid = turned("max_mid", ["bank_b"], ["wg0", "codes0_00"], weight(2, 1, 2 * P), 2 * P, max_with(tanh_mid))
         rec = {b: turn_back(b, b - 2, 2 * P, (h3_mid, max_mid), gain_nat[:, b : b + 1], None) for b in (2, 3)}
         before3 = sb("before3", [P, M], F32, tag="tanh_mid1")
         fetch_before(before3[:], 3)
         new_operands(3, W1[:1], KP, "tanh_mid0")
-        quantise(3, W1[:1], KP)
+        quantise(3, W1[:1], KP, tag="wg1")
         put(2, rec[2][:], wgs_nat[:])
         new_operands(3, W1[1:], KP, "rec2")
-        tag = quantise(3, W1[1:], KP)
-        tanh_tags = ["raw1_00", "raw1_01", "raw1_10", "raw2_00"]
-        tanh_hi = turned("tanh_hi", ["bank_a"], tanh_tags, weight(3, 0, KP), KP, tanh_out)
+        tag = quantise(3, W1[1:], KP, tag="codes0_00")
         x2 = sb("x2", [P, M], F32, tag=tag)
         fetch_difference(x2[:], 2, whole)
         x_lo[2] = x2[:]
         put(3, rec[3][:], wgs_nat[:])
 
         new_operands(3, W2, KP, "rec3")
-        quantise(3, W2[:1], KP)
-        tag = quantise(3, W2[1:], KP)
+        tag = quantise(3, W2, KP, tag="wg0")
+        tanh_tags = ["raw3_11", "raw1_01", "raw1_10", "raw2_00"]
+        tanh_hi = turned("tanh_hi", ["bank_a"], tanh_tags, weight(3, 0, KP), KP, tanh_out)
+        h3_hi = turned("h3_hi", ["bank_s"], ["raw0_00", "raw0_01", "raw0_10", "raw0_11"], weight3(KP, KP), KP, copy_out)
         close_slice(3, tag)
         max_tags = ["raw1_11", "raw2_01", "raw2_10", "raw2_11"]
         max_hi = turned("max_hi", ["bank_b", "bank_a"], max_tags, weight(3, 1, KP), KP, max_with(tanh_hi))
@@ -349,13 +343,24 @@ def tile_list_waterhole_redistribution_features_kernel(
         rec_tags = ["rec0", "rec1", "rec2", "raw3_00"]
         for t in range(PACK - 1):
             rec[4 + t] = turn_back(4 + t, t, KP, (h3_hi, max_hi), gain_dealt[:, t : t + 1], rec_tags[t])
-        x0_bf = sb("x0_bf", [P, PACK * M], BF16, tag="stage3_00")
+        x0_bf = sb("x0_bf", [P, PACK * M], BF16, tag="wg1")
         interleave(nc.scalar.copy, x0_bf[:], x_moved[:])
         rec[7] = turn_back(7, 3, KP, (h3_hi, max_hi), gain_dealt[:, 3:4], rec_tags[3])
 
         before_hi = sb("before_hi", [P, PACK - 1, M], F32, tag=tanh_tags[3])
         for n in range(PACK - 1):
             fetch_before(before_hi[:, n, :], 5 + n)
+
+        w4_codes = sb("w4_codes", [P, PASSES, PACK, P], I32, tag="tanh0")
+        nc.vector.tensor_copy(
+            out=w4_codes[:].rearrange("p a t q -> p a q t"),
+            in_=w4_raw[:].rearrange("p a (q t) -> p a q t", t=PACK),
+        )
+        w4_dealt = sb("w4_dealt", [P, PASSES, PACK, P], U8, tag=tag_w1)
+        nc.vector.tensor_copy(
+            out=w4_dealt[:],
+            in_=w4_plane[:].rearrange("p a (q t) -> p a t q", t=PACK),
+        )
 
         x_hi = sb("x_hi", [P, PACK, M], F32, tag="raw3_01")
         put(4, rec[4][:], wgs_dealt[:, 0, :])

from contextlib import ExitStack

import concourse.mybir as mybir
from concourse.masks import make_identity

K, T, S, H, T2, M, N = 1024, 2048, 512, 1024, 1024, 512, 512
FLOPS = 2 * (3 * K * H * S + H * N * M)

F32 = mybir.dt.float32
BF16 = mybir.dt.bfloat16
I32 = mybir.dt.int32
U32 = mybir.dt.uint32
U16 = mybir.dt.uint16
U8 = mybir.dt.uint8
FP8X4 = mybir.dt.float8_e4m3fn_x4
FP4X4 = mybir.dt.float4_e2m1fn_x4
ALU = mybir.AluOpType
ACT = mybir.ActivationFunctionType

P = 128
PACK = 4
KP = P * PACK
PASSES = K // KP
QUAD = 32
HALF_M = M // 2


def tile_list_waterhole_redistribution_features_kernel(
    tc, tab_words, tab_scales, offs, offs2, offs3, offs4, w1, w2, w3_words, w3_scales,
    gain, wgs, page0, w4_words, w4_scales, b4, out_0, out_1, out_2,
):
    nc = tc.nc
    with ExitStack() as ctx:
        lists = ctx.enter_context(tc.tile_pool(name="lists", bufs=1))
        pool = ctx.enter_context(tc.tile_pool(name="sbuf", bufs=1))
        psum = ctx.enter_context(tc.psum_pool(name="psum", bufs=2))

        def sb(name, shape, dtype, tag=None):
            return pool.tile(shape, dtype, name=name, tag=tag or name, align_bytes=64)

        def bank(name, tag, shape):
            return psum.tile(shape, F32, name=name, tag=tag)

        def load_list(name, src):
            t = lists.tile([P, S // 16], U16, name=name)
            nc.sync.dma_start(t[:], src)
            return t

        def load_weight_piece(name, w, a, col0, width):
            raw = sb(name, [P, PACK, width], F32)
            rows = w[a * KP : (a + 1) * KP, col0 : col0 + width]
            nc.sync.dma_start(out=raw[:], in_=rows.rearrange("(p j) c -> p j c", j=PACK))
            return raw

        def load_page(name, rows):
            t = sb(name, [P, T2], F32)
            nc.sync.dma_start(out=t[:], in_=rows)
            return t

        def zero_plane(engine, name, width, tag=None):
            plane = sb(name, [P, PASSES, width], U8, tag=tag)
            engine.memset(plane[:].bitcast(I32), 0)
            return plane

        def load_scales(queue, plane, src):
            for q in range(P // QUAD):
                queue.dma_start(
                    out=plane[QUAD * q : QUAD * q + 4, :, :].bitcast(I32),
                    in_=src[:, 4 * q : 4 * q + 4, :].rearrange("a r c -> r a c").bitcast(I32),
                )

        def interleave(engine_copy, dst, src):
            engine_copy(
                out=dst.rearrange("p (c i t) -> p c t i", i=4, t=PACK),
                in_=src.rearrange("p t (c i) -> p c t i", i=4),
            )

        tab_plane = zero_plane(nc.gpsimd, "tab_plane", T)
        w3_plane = zero_plane(nc.vector, "w3_plane", H)
        gain_rows = sb("gain_rows", [P, P], F32)
        nc.gpsimd.memset(gain_rows[:], 0.0)
        nc.gpsimd.dma_start(out=gain_rows[0:PACK, :], in_=gain[0:KP].rearrange("(b p) -> b p", p=P))
        load_scales(nc.scalar, tab_plane, tab_scales)
        load_scales(nc.gpsimd, w3_plane, w3_scales)

        def load_table(a):
            t = sb(f"tabw{a}", [P, T], I32)
            nc.sync.dma_start(out=t[:], in_=tab_words[a].rearrange("p c i -> p (c i)").bitcast(I32))
            return t

        raw = {}

        W1, W2 = [(0, 0), (0, 1)], [(1, 0), (1, 1)]

        def load_chunk(c, pieces, col0, width):
            for wi, a in pieces:
                raw[c, wi, a] = load_weight_piece(f"raw{c}_{wi}{a}", (w1, w2)[wi], a, col0, width)

        def load_w3(name, col0):
            t = sb(name, [P, PASSES, 2 * KP], U8)
            src = w3_words[:, :, 2 * col0 : 2 * (col0 + KP)].rearrange("a p c -> p a c")
            nc.sync.dma_start(out=t[:].bitcast(I32), in_=src.bitcast(I32))
            return t

        idx = load_list("idx", offs)
        load_chunk(0, W1, 0, P)
        tabw = [load_table(0)]
        load_chunk(0, W2, 0, P)
        tabw.append(load_table(1))
        w3_codes = [load_w3("w3_lo", 0)]
        idx4 = load_list("idx4", offs4)
        page = [load_page("page0", page0[0:P, :])]
        wgs_nat = sb("wgs_nat", [P, S], F32)
        nc.sync.dma_start(out=wgs_nat[:], in_=wgs)
        idx2 = load_list("idx2", offs2)
        load_chunk(1, W1 + W2, P, P)
        idx3 = load_list("idx3", offs3)
        page.append(load_page("page1", page0[P : 2 * P, :]))
        load_chunk(2, W1 + W2, 2 * P, 2 * P)
        page.append(load_page("page2", page0[2 * P : 3 * P, :]))
        load_chunk(3, W1[:1], KP, KP)
        page.append(load_page("page3", page0[3 * P : 4 * P, :]))
        load_chunk(3, W1[1:] + W2, KP, KP)
        w3_codes.append(load_w3("w3_hi", KP))
        w4_raw = sb("w4_raw", [P, PASSES, N], I32)
        nc.sync.dma_start(out=w4_raw[:], in_=w4_words.rearrange("a p c i -> p a (c i)").bitcast(I32))
        page_hi = page0[KP:H, :].rearrange("(p t) c -> p t c", t=PACK)
        page.append(load_page("page4", page_hi[:, 0, :]))
        wgs_dealt = sb("wgs_dealt", [P, PACK, S], F32)
        for q in range(P // QUAD):
            nc.sync.dma_start(
                out=wgs_dealt[QUAD * q : QUAD * (q + 1), :, :],
                in_=wgs.rearrange("(q t) j -> q t j", t=PACK),
            )
        for t in range(1, PACK):
            page.append(load_page(f"page{4 + t}", page_hi[:, t, :]))
        gain_dealt = sb("gain_dealt", [P, PACK], F32)
        nc.sync.dma_start(out=gain_dealt[:], in_=gain[KP:H].rearrange("(p t) -> p t", t=PACK))
        b4_dealt = sb("b4_dealt", [P, PACK], F32)
        nc.sync.dma_start(out=b4_dealt[:], in_=b4.rearrange("(p t) -> p t", t=PACK))

        ident = sb("ident", [P, P], F32)
        make_identity(nc, ident[:])
        gain_turned = bank("gain_turned", "bank_s", [P, P])
        nc.tensor.transpose(gain_turned[:], gain_rows[:], ident[:])
        gain_nat = sb("gain_nat", [P, PACK], F32)
        nc.scalar.copy(out=gain_nat[:], in_=gain_turned[:, 0:PACK])

        vw, vs = [], []
        for a in range(PASSES):
            s_t = sb(f"vs{a}", [P, S], U8)
            nc.vector.tensor_copy(s_t[:], tab_plane[:, a, :].indirect(idx[:]))
            w_t = sb(f"vw{a}", [P, S], U32)
            nc.vector.tensor_copy(w_t[:], tabw[a][:].bitcast(U32).indirect(idx[:]))
            vw.append(w_t)
            vs.append(s_t)

        operands = {}

        def new_operands(c, pieces, width, tag):
            name = f"{c}_{pieces[0][0]}{pieces[0][1]}"
            words = sb(f"codes{name}", [P, len(pieces) * width], U32, tag=tag)
            plane = sb(f"plane{name}", [P, len(pieces) * width], U8)
            for n, piece in enumerate(pieces):
                operands[(c,) + piece] = (words, plane, n * width)

        def quantise(c, pieces, width, tag=None):
            tag = tag or f"stage{c}_{pieces[0][0]}{pieces[0][1]}"
            stage = sb(f"stage{c}_{pieces[0][0]}{pieces[0][1]}", [P, len(pieces), PACK * width], BF16, tag=tag)
            for n, (wi, a) in enumerate(pieces):
                interleave(nc.scalar.copy, stage[:, n, :], raw[c, wi, a][:])
            words, plane, start = operands[(c,) + pieces[0]]
            span = slice(start, start + len(pieces) * width)
            nc.vector.quantize_mx(
                out=words[:, span].bitcast(FP8X4), scales=plane[:, span], in_=stage[:].rearrange("p n c -> p (n c)")
            )
            return tag

        def product(out, stationary, moving):
            for a in range(PASSES):
                lw, ls = stationary(a)
                rw, rs = moving(a)
                nc.tensor.matmul_mx(
                    out=out, lhsT=lw, lhsT_scale=ls, rhs=rw, rhs_scale=rs,
                    start=(a == 0), stop=(a == PASSES - 1),
                )

        def table(cols):
            return lambda a: (vw[a][:, cols].bitcast(FP8X4), vs[a][:, cols])

        def weight(c, wi, width):
            def operand(a):
                words, plane, start = operands[c, wi, a]
                return words[:, start : start + width].bitcast(FP8X4), plane[:, start : start + width]

            return operand

        def weight3(col0, width):
            return lambda a: (
                w3_codes[col0 // KP][:, a, 2 * (col0 % KP) : 2 * (col0 % KP + width)].bitcast(FP4X4),
                w3_plane[:, a, col0 : col0 + width],
            )

        def fetch_before(dst, b):
            nc.vector.tensor_copy(dst, page[b][:].indirect(idx4[:]))
            before[b] = dst

        def fetch_difference(dst, b, cols):
            picks = idx3[:, cols.start // 16 : cols.stop // 16]
            nc.vector.tensor_tensor(dst, page[b][:].indirect(picks), before[b][:, cols], ALU.subtract)

        def put(b, records, weights):
            nc.vector.tensor_tensor(page[b][:].indirect(idx2[:]), records, weights, ALU.mult)

        before = {}
        x_lo = {}
        whole = slice(0, S)

        def direct_products(b, tanh_tag):
            h1 = bank(f"h1_{b}", "bank_a", [P, S])
            product(h1[:], weight(b, 0, P), table(whole))
            h2 = bank(f"h2_{b}", "bank_b", [P, S])
            product(h2[:], weight(b, 1, P), table(whole))
            h3 = bank(f"h3_{b}", "bank_c", [P, S])
            product(h3[:], weight3(P * b, P), table(whole))
            th = sb(f"tanh{b}", [P, S], F32, tag=tanh_tag)
            nc.scalar.activation(th[:], h1[:], ACT.Tanh)
            wg = sb(f"wg{b}", [P, S], F32)
            nc.scalar.activation(wg[:], wgs_nat[:], ACT.Copy, scale=gain_nat[:, b : b + 1])
            return th, h2, h3, wg

        def direct_put(b, th, h2, h3, wg):
            rec = sb(f"rec{b}", [P, S], F32)
            larger = sb(f"larger{b}", [P, S], F32)
            nc.vector.tensor_tensor(larger[:], th[:], h2[:], ALU.max)
            nc.vector.tensor_tensor(rec[:], larger[:], h3[:], ALU.add)
            put(b, rec[:], wg[:])

        def turned(name, bank_tags, tile_tags, moving, width, finish):
            per_bank = KP // width
            tiles = []
            for n, tile_tag in enumerate(tile_tags):
                acc = bank(f"{name}_acc{n}", bank_tags[n % len(bank_tags)], [P, KP])
                for m in range(per_bank):
                    jb = per_bank * n + m
                    product(acc[:, width * m : width * (m + 1)], table(slice(P * jb, P * (jb + 1))), moving)
                dst = sb(f"{name}{n}", [P, KP], F32, tag=tile_tag)
                if per_bank == 1:
                    finish(n, dst[:].rearrange("p (t q) -> p t q", t=PACK), acc[:].rearrange("p (q t) -> p t q", t=PACK))
                else:
                    finish(n, dst[:], acc[:])
                tiles.append(dst)
            return tiles

        def copy_out(n, dst, acc):
            nc.scalar.copy(out=dst, in_=acc)

        def tanh_out(n, dst, acc):
            nc.scalar.activation(dst, acc, ACT.Tanh)

        def max_with(tanh_tiles):
            def finish(n, dst, acc):
                th = tanh_tiles[n][:]
                if len(dst.shape) == 3:
                    th = th.rearrange("p (t q) -> p t q", t=PACK)
                nc.vector.tensor_tensor(dst, th, acc, ALU.max)

            return finish

        def turn_back(b, s, width, terms, gain_col, tag):
            per_bank = KP // width
            acc = bank(f"sum{b}", "bank_s", [P, S])
            steps = [(tiles, jb) for tiles in terms for jb in range(S // P)]
            for n, (tiles, jb) in enumerate(steps):
                col0 = (jb % per_bank) * width + P * s
                nc.tensor.matmul(
                    acc[:, P * jb : P * (jb + 1)], tiles[jb // per_bank][:, col0 : col0 + P], ident[:],
                    start=(n == 0), stop=(n == len(steps) - 1), is_transpose=True,
                )
            rec = sb(f"rec{b}", [P, S], F32, tag=tag)
            nc.scalar.activation(rec[:], acc[:], ACT.Copy, scale=gain_col)
            return rec

        def close_slice(b, tag):
            pair = sb(f"pair{b}", [P, 2, M], F32, tag=tag)
            fetch_difference(pair[:, 0, :], b, whole)
            fetch_before(pair[:, 1, :], b + 1)
            x_lo[b] = pair[:, 0, :]

        new_operands(0, W1 + W2, P, None)
        for piece in W1 + W2:
            quantise(0, [piece], P)
        parts = direct_products(0, "tanh0")
        before0 = sb("before0", [P, M], F32)
        fetch_before(before0[:], 0)
        direct_put(0, *parts)

        w4_plane = zero_plane(nc.vector, "w4_plane", N, tag="stage0_11")
        load_scales(nc.gpsimd, w4_plane, w4_scales)

        new_operands(1, W1 + W2, P, "larger0")
        quantise(1, W1, P, tag="tanh0")
        tag = quantise(1, W2, P)
        parts = direct_products(1, None)
        close_slice(0, tag)
        direct_put(1, *parts)

        h3_mid = turned("h3_mid", ["bank_s"], ["stage0_00", "stage0_01"], weight3(2 * P, 2 * P), 2 * P, copy_out)

        new_operands(2, W1 + W2, 2 * P, "larger1")
        tag_w1 = quantise(2, W1, 2 * P, tag="before0")
        tag = quantise(2, W2, 2 * P, tag="tanh1")
        tanh_mid = turned("tanh_mid", ["bank_a"], ["tanh_mid0", "tanh_mid1"], weight(2, 0, 2 * P), 2 * P, tanh_out)
        close_slice(1, tag)
        max_mid = turned("max_mid", ["bank_b"], ["wg0", "codes0_00"], weight(2, 1, 2 * P), 2 * P, max_with(tanh_mid))
        rec = {b: turn_back(b, b - 2, 2 * P, (h3_mid, max_mid), gain_nat[:, b : b + 1], None) for b in (2, 3)}
        before3 = sb("before3", [P, M], F32, tag="tanh_mid1")
        fetch_before(before3[:], 3)
        new_operands(3, W1[:1], KP, "tanh_mid0")
        quantise(3, W1[:1], KP, tag="wg1")
        put(2, rec[2][:], wgs_nat[:])
        new_operands(3, W1[1:], KP, "rec2")
        tag = quantise(3, W1[1:], KP, tag="codes0_00")
        x2 = sb("x2", [P, M], F32, tag=tag)
        fetch_difference(x2[:], 2, whole)
        x_lo[2] = x2[:]
        put(3, rec[3][:], wgs_nat[:])

        new_operands(3, W2, KP, "rec3")
        tag = quantise(3, W2, KP, tag="wg0")
        tanh_tags = ["raw3_11", "raw1_01", "raw1_10", "raw2_00"]
        tanh_hi = turned("tanh_hi", ["bank_a"], tanh_tags, weight(3, 0, KP), KP, tanh_out)
        h3_hi = turned("h3_hi", ["bank_s"], ["raw0_00", "raw0_01", "raw0_10", "raw0_11"], weight3(KP, KP), KP, copy_out)
        close_slice(3, tag)
        max_tags = ["raw1_11", "raw2_01", "raw2_10", "raw2_11"]
        max_hi = turned("max_hi", ["bank_b", "bank_a"], max_tags, weight(3, 1, KP), KP, max_with(tanh_hi))

        x_moved = sb("x_moved", [P, PACK, M], F32, tag="raw3_00")
        for b in range(PACK):
            for t in range(PACK):
                nc.sync.dma_start(out=x_moved[QUAD * b : QUAD * (b + 1), t, :], in_=x_lo[b][t:P:PACK, :])

        rec_tags = ["rec0", "rec1", "rec2", "raw3_00"]
        for t in range(PACK - 1):
            rec[4 + t] = turn_back(4 + t, t, KP, (h3_hi, max_hi), gain_dealt[:, t : t + 1], rec_tags[t])
        x0_bf = sb("x0_bf", [P, PACK * M], BF16, tag="wg1")
        interleave(nc.scalar.copy, x0_bf[:], x_moved[:])
        rec[7] = turn_back(7, 3, KP, (h3_hi, max_hi), gain_dealt[:, 3:4], rec_tags[3])

        before_hi = sb("before_hi", [P, PACK - 1, M], F32, tag=tanh_tags[3])
        for n in range(PACK - 1):
            fetch_before(before_hi[:, n, :], 5 + n)

        w4_codes = sb("w4_codes", [P, PASSES, PACK, P], I32, tag="tanh0")
        nc.vector.tensor_copy(
            out=w4_codes[:].rearrange("p a t q -> p a q t"),
            in_=w4_raw[:].rearrange("p a (q t) -> p a q t", t=PACK),
        )
        w4_dealt = sb("w4_dealt", [P, PASSES, PACK, P], U8, tag=tag_w1)
        nc.vector.tensor_copy(
            out=w4_dealt[:],
            in_=w4_plane[:].rearrange("p a (q t) -> p a t q", t=PACK),
        )

        x_hi = sb("x_hi", [P, PACK, M], F32, tag="raw3_01")
        put(4, rec[4][:], wgs_dealt[:, 0, :])
        for t in range(PACK - 1):
            put(5 + t, rec[5 + t][:], wgs_dealt[:, t + 1, :])
            fetch_difference(x_hi[:, t, :], 4 + t, whole)

        x0_codes = sb("x0_codes", [P, M], U32, tag=rec_tags[3])
        x0_plane = sb("x0_plane", [P, M], U8)
        nc.vector.quantize_mx(out=x0_codes[:].bitcast(FP8X4), scales=x0_plane[:], in_=x0_bf[:])

        def y_pass(acc, a, tp, x_codes, x_plane):
            for n in range(2):
                t = 2 * tp + n
                nc.tensor.matmul_mx(
                    out=acc[:, n, :],
                    lhsT=w4_codes[:, a, t, :].bitcast(FP8X4), lhsT_scale=w4_dealt[:, a, t, :],
                    rhs=x_codes.bitcast(FP8X4), rhs_scale=x_plane,
                    start=(a == 0 and n == 0), stop=(a == PASSES - 1 and n == 1),
                )

        y_banks = {}
        for hf in range(2):
            cols = slice(HALF_M * hf, HALF_M * (hf + 1))
            for tp in range(2):
                acc = bank(f"y_{hf}{tp}", ("bank_c", "bank_b")[hf], [P, 2, HALF_M])
                y_pass(acc, 0, tp, x0_codes[:, cols], x0_plane[:, cols])
                y_banks[hf, tp] = acc

        for hf in range(2):
            cols = slice(HALF_M * hf, HALF_M * (hf + 1))
            fetch_difference(x_hi[:, PACK - 1, cols], 7, cols)

        y_rows = out_0.rearrange("(p t) m -> p t m", t=PACK)
        y_plane = sb("y_plane", [P, M], U8)
        for hf in range(2):
            cols = slice(HALF_M * hf, HALF_M * (hf + 1))
            x_bf = sb(f"x1_bf{hf}", [P, PACK * HALF_M], BF16)
            interleave((nc.scalar.copy, nc.vector.tensor_copy)[hf], x_bf[:], x_hi[:, :, cols])
            x_codes = sb(f"x1_codes{hf}", [P, HALF_M], U32)
            x_plane = sb(f"x1_plane{hf}", [P, HALF_M], U8)
            nc.vector.quantize_mx(out=x_codes[:].bitcast(FP8X4), scales=x_plane[:], in_=x_bf[:])
            y = sb(f"y{hf}", [P, PACK, HALF_M], F32, tag=f"raw3_1{hf}")
            for tp in range(2):
                acc = y_banks[hf, tp]
                y_pass(acc, 1, tp, x_codes[:], x_plane[:])
                for n in range(2):
                    t = 2 * tp + n
                    if tp == 0:
                        nc.scalar.activation(y[:, t, :], acc[:, n, :], ACT.Identity, bias=b4_dealt[:, t : t + 1])
                    else:
                        nc.vector.tensor_scalar(y[:, t, :], acc[:, n, :], b4_dealt[:, t : t + 1], None, ALU.add)
            nc.sync.dma_start(out=y_rows[:, :, cols], in_=y[:])
            y_bf = sb(f"y_bf{hf}", [P, PACK * HALF_M], BF16)
            interleave(nc.vector.tensor_copy, y_bf[:], y[:])
            y_codes = sb(f"y_codes{hf}", [P, HALF_M], I32)
            nc.vector.quantize_mx(out=y_codes[:].bitcast(FP8X4), scales=y_plane[:, cols], in_=y_bf[:])
            nc.scalar.dma_start(
                out=out_1[0, :, cols, :].rearrange("p m t -> p (m t)").bitcast(I32), in_=y_codes[:]
            )
        for q in range(P // QUAD):
            (nc.sync, nc.scalar)[q % 2].dma_start(
                out=out_2[0, 4 * q : 4 * q + 4, :].bitcast(I32),
                in_=y_plane[QUAD * q : QUAD * q + 4, :].bitcast(I32),
            )
